import numpy as np
import ml_dtypes


def mxq(x, axis, fmt="e4m3"):
    dtype, down = {"e4m3": (ml_dtypes.float8_e4m3fn, 7), "e5m2": (ml_dtypes.float8_e5m2, 14)}[fmt]
    v = np.moveaxis(np.asarray(x, np.float32).astype(ml_dtypes.bfloat16).astype(np.float64), axis, -1)
    blocks = v.reshape(v.shape[:-1] + (-1, 32))
    amax = np.abs(blocks).max(-1, keepdims=True)
    byte = np.maximum(np.where(amax > 0, np.frexp(amax)[1] - 1 + 127, 0) - down, 1)
    scale = np.exp2(byte - 127.0)
    codes = (blocks / scale).astype(np.float32).astype(dtype).astype(np.float64)
    return np.moveaxis((codes * scale).reshape(v.shape), -1, axis)


WIDE = False


def mx_kscale(k):
    if not WIDE:
        return np.ones(k)
    levels = np.array([10, -10, 5, -5, 0])
    if k % 512:
        return np.exp2(np.random.permutation(np.resize(levels, k // 32))).repeat(32)
    a = np.empty((k // 512, 16))
    for p in range(k // 512):
        a[p, :8] = np.random.permutation(np.resize(levels, 8))
        for g in range(8):
            far = levels[np.abs(levels - a[p, g]) >= 10]
            a[p, g + 8] = far[np.random.randint(len(far))]
    return np.exp2(a.ravel()).repeat(32)


def f64(x):
    return np.asarray(x).astype(np.float64)


def striped(idx):
    return np.tile(np.asarray(idx).reshape(-1, 16).T, (8, 1)).astype(np.uint16)


def unstriped(offs):
    return offs[:16].T.reshape(-1).astype(np.int64)


E2M1 = np.array([0.0, 0.5, 1.0, 1.5, 2.0, 3.0, 4.0, 6.0, -0.0, -0.5, -1.0, -1.5, -2.0, -3.0, -4.0, -6.0])


def pack_weight(w, fmt):
    k, n = w.shape
    w = f64(np.asarray(w, np.float32).astype(ml_dtypes.bfloat16)).reshape(k // 32, 32, n)
    amax = np.abs(w).max(1)
    if fmt == "e4m3":
        byte = np.frexp(amax)[1] - 1 + 127 - 7
    else:
        mant, ex = np.frexp(amax / 6.0)
        byte = np.where(mant > 0.5, ex, ex - 1) + 127
    byte = np.clip(np.where(amax > 0, byte, 1), 1, 254)
    scaled = (w * np.exp2(127.0 - byte)[:, None, :]).reshape(k, n).astype(np.float32)
    by_word = np.ascontiguousarray(scaled.reshape(k // 512, 128, 4, n).transpose(0, 1, 3, 2))
    if fmt == "e4m3":
        words = by_word.astype(ml_dtypes.float8_e4m3fn).view(np.uint8)
    else:
        c = by_word.astype(ml_dtypes.float4_e2m1fn).view(np.uint8) & 0xF
        words = (c[..., 0::2] | (c[..., 1::2] << 4)).reshape(k // 512, 128, 2 * n)
    return np.ascontiguousarray(words), np.ascontiguousarray(byte.astype(np.uint8).reshape(k // 512, 16, n))


def unpack_weight(words, scales, fmt):
    g, _, n = scales.shape
    words = np.ascontiguousarray(words).reshape(g, 128, n, -1)
    if fmt == "e4m3":
        vals = words.view(ml_dtypes.float8_e4m3fn).astype(np.float64)
    else:
        nib = np.empty((g, 128, n, 4), np.uint8)
        nib[..., 0::2] = words & 0xF
        nib[..., 1::2] = words >> 4
        vals = E2M1[nib]
    vals = vals * np.repeat(np.exp2(scales.astype(np.float64) - 127.0), 8, axis=1)[..., None]
    return vals.transpose(0, 1, 3, 2).reshape(g * 512, n)


D, E, T, I, Q = 512, 512, 2048, 512, 128


def setup_inputs():
    n = np.random.standard_normal
    idx = np.random.permutation(T)[:I]
    fd = mx_kscale(D)
    fe = mx_kscale(E)
    fi = mx_kscale(I)
    ti = np.ones(T)
    ti[idx] = fi
    keysp = pack_weight(n((D, T)) / fd[:, None], "e2m1")
    valsp = pack_weight(n((E, T)) / fe[:, None], "e2m1")
    return {
        "query": (n((D, Q)) * 0.4 / np.sqrt(D) * fd[:, None]).astype(np.float32),
        "query2": (n((D, Q)) * 0.6 / np.sqrt(D) * fd[:, None]).astype(np.float32),
        "keys_words": keysp[0],
        "keys_scales": keysp[1],
        "l1": (np.random.uniform(6.2, 6.5, (Q, 1))).astype(np.float32),
        "l2": (np.random.uniform(6.2, 6.5, (Q, 1))).astype(np.float32),
        "floor": (np.random.uniform(0.0005, 0.002, (Q, 1))).astype(np.float32),
        "gout": (n((E, Q)) * 1 / np.sqrt(E) * fe[:, None]).astype(np.float32),
        "vals_words": valsp[0],
        "vals_scales": valsp[1],
        "size": (np.random.uniform(0.5, 2.0, (1, I))).astype(np.float32),
        "fs": (np.random.uniform(1.0, 4.0, (1, I)) * fi).astype(np.float32),
        "keyrows": (n((D, T)) / ti).astype(np.float32),
        "res": (n((Q, D)) * 4.0).astype(np.float32),
        "offs": striped(idx),
    }


def reference(query, query2, keys_words, keys_scales, l1, l2, floor, gout, vals_words, vals_scales, size, fs, keyrows, res, offs):
    idx = unstriped(offs)
    keysu = unpack_weight(keys_words, keys_scales, "e2m1")
    valsu = unpack_weight(vals_words, vals_scales, "e2m1")
    queryq = mxq(f64(query), 0, "e4m3")
    keysidxg = keysu[:, idx]
    a = queryq.T @ keysidxg
    query2q = mxq(f64(query2), 0, "e4m3")
    b = query2q.T @ keysidxg
    pa = np.exp(a - f64(l1))
    pb = np.exp(b - f64(l2))
    goutq = mxq(f64(gout), 0, "e4m3")
    valsidxg = valsu[:, idx]
    c0 = goutq.T @ valsidxg
    dpb = c0 * f64(size) * pa / np.square(pb + f64(floor)) * (-1.0)
    db = dpb * pb
    gs = db * f64(fs)
    gt1 = gs.T
    kt = f64(keyrows)[:, idx].T
    gt1q = mxq(gt1, 0, "e4m3")
    ktq = mxq(kt, 0, "e4m3")
    gq = gt1q.T @ ktq
    y = gq + f64(res)
    return y

@@ -1,0 +1,168 @@
+from contextlib import ExitStack
+
+import concourse.mybir as mybir
+from concourse.masks import make_identity
+
+D, E, T, I, Q = 512, 512, 2048, 512, 128
+FLOPS = 2 * Q * I * (D + D + E + D)
+
+F32 = mybir.dt.float32
+BF16 = mybir.dt.bfloat16
+I32 = mybir.dt.int32
+U32 = mybir.dt.uint32
+U16 = mybir.dt.uint16
+U8 = mybir.dt.uint8
+FP8X4 = mybir.dt.float8_e4m3fn_x4
+FP4X4 = mybir.dt.float4_e2m1fn_x4
+ACT = mybir.ActivationFunctionType
+ALU = mybir.AluOpType
+
+P = 128
+PACK = 4
+CHUNKS = D // P
+
+
+def tile_attend_bclippedratio_b_q_kernel(tc, query, query2, keys_words, keys_scales, l1, l2, floor, gout,
+                                          vals_words, vals_scales, size, fs, keyrows, res, offs, out):
+    nc = tc.nc
+    with ExitStack() as ctx:
+        sb = ctx.enter_context(tc.tile_pool(name="sb", bufs=1))
+        ps = ctx.enter_context(tc.psum_pool(name="ps", bufs=1))
+
+        def tile(name, shape, dtype, tag=None):
+            return sb.tile(shape, dtype, name=name, tag=tag or name, align_bytes=64)
+
+        offsets = sb.tile([P, I // 16], U16, name="offsets")
+        nc.sync.dma_start(offsets[:], offs)
+
+        def load_scales(name, scales, zeroing, queue):
+            plane = tile(name, [P, T], U8)
+            zeroing.memset(plane[:].bitcast(I32), 0)
+            for r in range(4):
+                queue.dma_start(plane[r:P:32, :].bitcast(I32), scales[0, r:16:4, :].bitcast(I32))
+            return plane
+
+        def load_words(name, words):
+            pool = tile(name, [P, T], U16)
+            nc.sync.dma_start(pool[:].bitcast(I32), words[0].bitcast(I32))
+            return pool
+
+        def load_columns(name, src):
+            raw = tile(name, [P, PACK, Q], F32)
+            nc.sync.dma_start(raw[:], src.rearrange("(p j) q -> p j q", j=PACK))
+            return raw
+
+        def load_small(name, src, queue):
+            small = tile(name, list(src.shape), F32)
+            queue.dma_start(small[:], src)
+            return small
+
+        size_col = load_small("size_col", size.rearrange("o (p r) -> (o p) r", r=PACK), nc.sync)
+        fs_col = load_small("fs_col", fs.rearrange("o (p r) -> (o p) r", r=PACK), nc.sync)
+        kw_pool = load_words("kw_pool", keys_words)
+        ks_pool = load_scales("ks_pool", keys_scales, nc.vector, nc.scalar)
+        q2_raw = load_columns("q2_raw", query2)
+        q1_raw = load_columns("q1_raw", query)
+        vw_pool = load_words("vw_pool", vals_words)
+        go_raw = load_columns("go_raw", gout)
+        l2_col = load_small("l2_col", l2, nc.gpsimd)
+        l1_col = load_small("l1_col", l1, nc.gpsimd)
+        floor_col = load_small("floor_col", floor, nc.gpsimd)
+        vs_pool = load_scales("vs_pool", vals_scales, nc.gpsimd, nc.sync)
+
+        ident = tile("ident", [P, P], F32)
+        make_identity(nc, ident[:])
+
+        neg_l2 = tile("neg_l2", [Q, 1], F32)
+        nc.gpsimd.tensor_scalar(neg_l2[:], l2_col[:], -1.0, 0.0, ALU.mult, ALU.add)
+        neg_l12 = tile("neg_l12", [Q, 1], F32)
+        nc.gpsimd.tensor_tensor(neg_l12[:], neg_l2[:], l1_col[:], ALU.subtract)
+        slot_w = tile("slot_w", [P, PACK], F32)
+        nc.gpsimd.tensor_tensor(slot_w[:], size_col[:], fs_col[:], ALU.mult)
+
+        def gather(name, pool, dtype):
+            picked = tile(name, [P, I], dtype)
+            nc.vector.tensor_copy(picked[:], pool[:].indirect(offsets[:]))
+            return picked
+
+        def interleave(name, raw):
+            grouped = tile(name, [P, Q, PACK], BF16)
+            nc.scalar.activation(grouped[:], raw[:].rearrange("p j q -> p q j"), ACT.Copy)
+            return grouped
+
+        def quantise(name, grouped):
+            codes = tile(name + "_codes", [P, P], U32)
+            scales = tile(name + "_scales", [P, P], U8)
+            nc.vector.quantize_mx(out=codes[:].bitcast(FP8X4), scales=scales[:],
+                                  in_=grouped[:].rearrange("p c j -> p (c j)"))
+            return codes, scales
+
+        def score(bank, rows, words, scales, start, stop):
+            nc.tensor.matmul_mx(out=bank[:], lhsT=rows[0][:].bitcast(FP8X4), lhsT_scale=rows[1][:],
+                                rhs=words[:].bitcast(FP4X4), rhs_scale=scales[:], start=start, stop=stop)
+
+        def dealt(bank):
+            return bank[:].rearrange("q (s r) -> q r s", r=PACK)
+
+        kw = gather("kw", kw_pool, U16)
+        ks = gather("ks", ks_pool, U8)
+        q2_mx = quantise("q2", interleave("q2_bf", q2_raw))
+        q1_mx = quantise("q1", interleave("q1_bf", q1_raw))
+        b_ps = ps.tile([Q, I], F32, name="b_ps")
+        ab_ps = ps.tile([Q, I], F32, name="ab_ps")
+        score(b_ps, q2_mx, kw, ks, True, True)
+        score(ab_ps, q2_mx, kw, ks, True, False)
+        score(ab_ps, q1_mx, kw, ks, False, True)
+
+        vw = gather("vw", vw_pool, U16)
+        vs = gather("vs", vs_pool, U8)
+        go_mx = quantise("go", interleave("go_bf", go_raw))
+        c0_ps = ps.tile([Q, I], F32, name="c0_ps")
+        score(c0_ps, go_mx, vw, vs, True, True)
+
+        kr_pools = []
+        for c, freed in enumerate(("q2_raw", "q1_raw", "go_raw", "vw_pool")):
+            kr = tile(f"kr_pool{c}", [P, T], F32, tag=freed)
+            nc.sync.dma_start(kr[:], keyrows[c * P:(c + 1) * P, :])
+            kr_pools.append(kr)
+        res_sb = tile("res_sb", [Q, D], F32, tag="vs_pool")
+        nc.sync.dma_start(res_sb[:], res)
+
+        pb = tile("pb", [Q, PACK, P], F32)
+        nc.scalar.activation(pb[:], dealt(b_ps), ACT.Exp, bias=neg_l2[:])
+        papb = tile("papb", [Q, PACK, P], F32)
+        nc.scalar.activation(papb[:], dealt(ab_ps), ACT.Exp, bias=neg_l12[:])
+        den = tile("den", [Q, PACK, P], F32)
+        nc.scalar.activation(den[:], pb[:], ACT.Square, bias=floor_col[:])
+        inv_abs = tile("inv_abs", [Q, PACK, P], F32)
+        nc.scalar.activation(inv_abs[:], den[:], ACT.Abs_reciprocal_sqrt)
+        inv_den = tile("inv_den", [Q, PACK, P], F32)
+        nc.scalar.activation(inv_den[:], inv_abs[:], ACT.Square)
+        ratio = tile("ratio", [Q, PACK, P], F32)
+        nc.vector.tensor_tensor(ratio[:], papb[:], inv_den[:], ALU.mult)
+        db = tile("db", [Q, PACK, P], F32)
+        nc.vector.scalar_tensor_tensor(db[:], dealt(c0_ps), -1.0, ratio[:], ALU.mult, ALU.mult)
+
+        dbt_ps = ps.tile([P, PACK, Q], F32, name="dbt_ps")
+        for r in range(PACK):
+            nc.tensor.transpose(dbt_ps[:, r, :], db[:, r, :], ident[:])
+        gt_bf = tile("gt_bf", [P, Q, PACK], BF16)
+        nc.vector.tensor_tensor(gt_bf[:], dbt_ps[:].rearrange("p r q -> p q r"),
+                                slot_w[:].unsqueeze(1).to_broadcast([P, Q, PACK]), ALU.mult)
+        gt_mx = quantise("gt", gt_bf)
+
+        for c in range(CHUNKS):
+            cols = slice(c * P, (c + 1) * P)
+            pairs = gather(f"kr{c}", kr_pools[c], BF16)[:].bitcast(F32)
+            kt_ps = ps.tile([P, 2, P], F32, name="kt_ps", bufs=2)
+            for u in range(2):
+                nc.tensor.transpose(kt_ps[:, u, :], pairs[:, u:I // 2:2], ident[:])
+            kt_bf = tile(f"kt_bf{c}", [P, P, PACK], BF16)
+            nc.scalar.copy(kt_bf[:].bitcast(F32), kt_ps[:].rearrange("p u d -> p d u"))
+            kt_mx = quantise(f"kt{c}", kt_bf)
+            gq_ps = ps.tile([Q, P], F32, name="gq_ps", bufs=2)
+            nc.tensor.matmul_mx(out=gq_ps[:], lhsT=gt_mx[0][:].bitcast(FP8X4), lhsT_scale=gt_mx[1][:],
+                                rhs=kt_mx[0][:].bitcast(FP8X4), rhs_scale=kt_mx[1][:], start=True, stop=True)
+            y = tile(f"y{c}", [Q, P], F32)
+            nc.vector.tensor_tensor(y[:], gq_ps[:], res_sb[:, cols], ALU.add)
+            nc.sync.dma_start(out[:, cols], y[:])

@@ -1,7 +1,6 @@
 from contextlib import ExitStack
 
 import concourse.mybir as mybir
-from concourse.masks import make_identity
 
 D, E, T, I, Q = 512, 512, 2048, 512, 128
 FLOPS = 2 * Q * I * (D + D + E + D)
@@ -21,78 +20,86 @@ P = 128
 PACK = 4
 CHUNKS = D // P
 
+POOL_BYTES = 4 * T
+ROWS_BYTES = 4 * I
+AT_KR0 = 0
+AT_KR1 = AT_KR0 + POOL_BYTES
+AT_KR2 = AT_KR1 + POOL_BYTES
+AT_PB = AT_KR2 + POOL_BYTES
+AT_KR3 = AT_PB + ROWS_BYTES
+AT_KR = [AT_KR0, AT_KR1, AT_KR2, AT_KR3]
+AT_Q1 = AT_KR1
+AT_GO = AT_PB - ROWS_BYTES // 2
+AT_GO_BF = AT_KR3 + POOL_BYTES - I
+AT_VW_POOL = AT_GO_BF + 2 * I
+AT_VS = AT_VW_POOL - I // 2
+AT_VS_POOL = AT_VW_POOL + 2 * T
+AT_SIZE = AT_VS_POOL + T
+AT_FS = AT_SIZE + 64
+AT_L2 = AT_FS + 64
+AT_L1 = AT_L2 + 64
+AT_FLOOR = AT_L1 + 64
+STAGED_BYTES = AT_FLOOR + 64
+AT_INV_ABS = STAGED_BYTES
+
 
 def tile_attend_bclippedratio_b_q_kernel(tc, query, query2, keys_words, keys_scales, l1, l2, floor, gout,
                                           vals_words, vals_scales, size, fs, keyrows, res, offs, out):
     nc = tc.nc
     with ExitStack() as ctx:
         sb = ctx.enter_context(tc.tile_pool(name="sb", bufs=1))
+        staged = ctx.enter_context(tc.tile_pool(name="staged", bufs=1))
         ps = ctx.enter_context(tc.psum_pool(name="ps", bufs=1))
 
-        def tile(name, shape, dtype, tag=None):
-            return sb.tile(shape, dtype, name=name, tag=tag or name, align_bytes=64)
+        def tile(name, shape, dtype, tag=None, at=None):
+            if at is None:
+                return sb.tile(shape, dtype, name=name, tag=tag or name, align_bytes=64)
+            return staged.tile(shape, dtype, name=name, align_bytes=64, offset=at)
 
         offsets = sb.tile([P, I // 16], U16, name="offsets")
         nc.sync.dma_start(offsets[:], offs)
 
-        def load_scales(name, scales, zeroing, queue):
-            plane = tile(name, [P, T], U8)
+        def load_scales(name, scales, zeroing, **place):
+            plane = tile(name, [P, T], U8, **place)
             zeroing.memset(plane[:].bitcast(I32), 0)
             for r in range(4):
-                queue.dma_start(plane[r:P:32, :].bitcast(I32), scales[0, r:16:4, :].bitcast(I32))
+                nc.sync.dma_start(plane[r:P:32, :].bitcast(I32), scales[0, r:16:4, :].bitcast(I32))
             return plane
 
-        def load_words(name, words):
-            pool = tile(name, [P, T], U16)
+        def load_words(name, words, **place):
+            pool = tile(name, [P, T], U16, **place)
             nc.sync.dma_start(pool[:].bitcast(I32), words[0].bitcast(I32))
             return pool
 
-        def load_columns(name, src):
-            raw = tile(name, [P, PACK, Q], F32)
+        def load_columns(name, src, **place):
+            raw = tile(name, [P, PACK, Q], F32, **place)
             nc.sync.dma_start(raw[:], src.rearrange("(p j) q -> p j q", j=PACK))
             return raw
 
-        def load_small(name, src, queue):
-            small = tile(name, list(src.shape), F32)
+        def load_small(name, src, queue, **place):
+            small = tile(name, list(src.shape), F32, **place)
             queue.dma_start(small[:], src)
             return small
 
-        size_col = load_small("size_col", size.rearrange("o (p r) -> (o p) r", r=PACK), nc.sync)
-        fs_col = load_small("fs_col", fs.rearrange("o (p r) -> (o p) r", r=PACK), nc.sync)
-        kw_pool = load_words("kw_pool", keys_words)
-        ks_pool = load_scales("ks_pool", keys_scales, nc.vector, nc.scalar)
-        q2_raw = load_columns("q2_raw", query2)
-        q1_raw = load_columns("q1_raw", query)
-        vw_pool = load_words("vw_pool", vals_words)
-        go_raw = load_columns("go_raw", gout)
-        l2_col = load_small("l2_col", l2, nc.gpsimd)
-        l1_col = load_small("l1_col", l1, nc.gpsimd)
-        floor_col = load_small("floor_col", floor, nc.gpsimd)
-        vs_pool = load_scales("vs_pool", vals_scales, nc.gpsimd, nc.sync)
+        def load_keyrows(c, **place):
+            pool = tile(f"kr_pool{c}", [P, T], F32, **place)
+            nc.sync.dma_start(pool[:], keyrows[c * P:(c + 1) * P, :])
+            return pool
 
-        ident = tile("ident", [P, P], F32)
-        make_identity(nc, ident[:])
-
-        neg_l2 = tile("neg_l2", [Q, 1], F32)
-        nc.gpsimd.tensor_scalar(neg_l2[:], l2_col[:], -1.0, 0.0, ALU.mult, ALU.add)
-        neg_l12 = tile("neg_l12", [Q, 1], F32)
-        nc.gpsimd.tensor_tensor(neg_l12[:], neg_l2[:], l1_col[:], ALU.subtract)
-        slot_w = tile("slot_w", [P, PACK], F32)
-        nc.gpsimd.tensor_tensor(slot_w[:], size_col[:], fs_col[:], ALU.mult)
-
-        def gather(name, pool, dtype):
-            picked = tile(name, [P, I], dtype)
+        def gather(name, pool, dtype, **place):
+            picked = tile(name, [P, I], dtype, **place)
             nc.vector.tensor_copy(picked[:], pool[:].indirect(offsets[:]))
             return picked
 
-        def interleave(name, raw):
-            grouped = tile(name, [P, Q, PACK], BF16)
+        def interleave(name, raw, **place):
+            grouped = tile(name, [P, Q, PACK], BF16, **place)
             nc.scalar.activation(grouped[:], raw[:].rearrange("p j q -> p q j"), ACT.Copy)
             return grouped
 
-        def quantise(name, grouped):
-            codes = tile(name + "_codes", [P, P], U32)
-            scales = tile(name + "_scales", [P, P], U8)
+        def quantise(name, grouped, at=None):
+            width = grouped.shape[1]
+            codes = tile(name + "_codes", [P, width], U32, at=at)
+            scales = tile(name + "_scales", [P, width], U8)
             nc.vector.quantize_mx(out=codes[:].bitcast(FP8X4), scales=scales[:],
                                   in_=grouped[:].rearrange("p c j -> p (c j)"))
             return codes, scales
@@ -104,65 +111,109 @@ def tile_attend_bclippedratio_b_q_kernel(tc, query, query2, keys_words, keys_sca
         def dealt(bank):
             return bank[:].rearrange("q (s r) -> q r s", r=PACK)
 
+        def turn_keyrows(c, pool, grouped, **place):
+            pairs = gather(f"kr{c}", pool, BF16, **place)[:].bitcast(F32)
+            kt_ps = ps.tile([P, 2, P], F32, name="kt_ps", bufs=2)
+            for u in range(2):
+                nc.tensor.transpose(kt_ps[:, u, :], pairs[:, u:I // 2:2], ident[:])
+            nc.scalar.copy(grouped.bitcast(F32), kt_ps[:].rearrange("p u d -> p d u"))
+
+        kw_pool = load_words("kw_pool", keys_words)
+        q2_raw = load_columns("q2_raw", query2)
+        zeros = tile("zeros", [P, STAGED_BYTES // 4], F32, at=0)
+        nc.vector.memset(zeros[:, :P], 0.0)
+        ident = tile("ident", [P, P], F32)
+        nc.gpsimd.affine_select(out=ident[:], in_=zeros[:, :P], compare_op=ALU.not_equal, fill=1.0, base=0,
+                                pattern=[[-1, P]], channel_multiplier=1)
+
+        ks_pool = load_scales("ks_pool", keys_scales, nc.vector)
+
+        q1_raw = load_columns("q1_raw", query, at=AT_Q1)
+        go_raw = load_columns("go_raw", gout, at=AT_GO)
+        vw_pool = load_words("vw_pool", vals_words, at=AT_VW_POOL)
+        l2_col = load_small("l2_col", l2, nc.sync, at=AT_L2)
+        l1_col = load_small("l1_col", l1, nc.sync, at=AT_L1)
+        floor_col = load_small("floor_col", floor, nc.sync, at=AT_FLOOR)
+        kr_pools = [load_keyrows(0, at=AT_KR[0])]
+        vs_pool = load_scales("vs_pool", vals_scales, nc.gpsimd, at=AT_VS_POOL)
+        size_col = load_small("size_col", size.rearrange("o (p r) -> (o p) r", r=PACK), nc.sync, at=AT_SIZE)
+        fs_col = load_small("fs_col", fs.rearrange("o (p r) -> (o p) r", r=PACK), nc.sync, at=AT_FS)
+
+        neg_l2 = tile("neg_l2", [Q, 1], F32)
+        nc.gpsimd.tensor_scalar(neg_l2[:], l2_col[:], -1.0, 0.0, ALU.mult, ALU.add)
+        neg_l12 = tile("neg_l12", [Q, 1], F32, at=AT_INV_ABS)
+        nc.gpsimd.tensor_tensor(neg_l12[:], neg_l2[:], l1_col[:], ALU.subtract)
+
         kw = gather("kw", kw_pool, U16)
         ks = gather("ks", ks_pool, U8)
         q2_mx = quantise("q2", interleave("q2_bf", q2_raw))
         q1_mx = quantise("q1", interleave("q1_bf", q1_raw))
+        kr_pools.append(load_keyrows(1, at=AT_KR[1]))
+
         b_ps = ps.tile([Q, I], F32, name="b_ps")
         ab_ps = ps.tile([Q, I], F32, name="ab_ps")
         score(b_ps, q2_mx, kw, ks, True, True)
         score(ab_ps, q2_mx, kw, ks, True, False)
         score(ab_ps, q1_mx, kw, ks, False, True)
 
-        vw = gather("vw", vw_pool, U16)
-        vs = gather("vs", vs_pool, U8)
-        go_mx = quantise("go", interleave("go_bf", go_raw))
+        go_mx = quantise("go", interleave("go_bf", go_raw, at=AT_GO_BF))
+        kr_pools.append(load_keyrows(2, at=AT_KR[2]))
+        kr_pools.append(load_keyrows(3, at=AT_KR[3]))
+        vw = gather("vw", vw_pool, U16, tag="q1_bf")
+        vs = gather("vs", vs_pool, U8, at=AT_VS)
+        slot_w = tile("slot_w", [P, PACK], F32, at=AT_VS_POOL)
+        nc.vector.tensor_tensor(slot_w[:], size_col[:], fs_col[:], ALU.mult)
         c0_ps = ps.tile([Q, I], F32, name="c0_ps")
         score(c0_ps, go_mx, vw, vs, True, True)
 
-        kr_pools = []
-        for c, freed in enumerate(("q2_raw", "q1_raw", "go_raw", "vw_pool")):
-            kr = tile(f"kr_pool{c}", [P, T], F32, tag=freed)
-            nc.sync.dma_start(kr[:], keyrows[c * P:(c + 1) * P, :])
-            kr_pools.append(kr)
-        res_sb = tile("res_sb", [Q, D], F32, tag="vs_pool")
+        res_sb = tile("res_sb", [Q, D], F32, tag="go_codes")
         nc.sync.dma_start(res_sb[:], res)
 
-        pb = tile("pb", [Q, PACK, P], F32)
+        pb = tile("pb", [Q, PACK, P], F32, at=AT_PB)
         nc.scalar.activation(pb[:], dealt(b_ps), ACT.Exp, bias=neg_l2[:])
         papb = tile("papb", [Q, PACK, P], F32)
         nc.scalar.activation(papb[:], dealt(ab_ps), ACT.Exp, bias=neg_l12[:])
         den = tile("den", [Q, PACK, P], F32)
         nc.scalar.activation(den[:], pb[:], ACT.Square, bias=floor_col[:])
-        inv_abs = tile("inv_abs", [Q, PACK, P], F32)
+        inv_abs = tile("inv_abs", [Q, PACK, P], F32, at=AT_INV_ABS)
         nc.scalar.activation(inv_abs[:], den[:], ACT.Abs_reciprocal_sqrt)
         inv_den = tile("inv_den", [Q, PACK, P], F32)
         nc.scalar.activation(inv_den[:], inv_abs[:], ACT.Square)
+
+        kt01_bf = tile("kt01_bf", [P, 2 * P, PACK], BF16, at=AT_INV_ABS)
+        turn_keyrows(0, kr_pools[0], kt01_bf[:, :P, :])
+
         ratio = tile("ratio", [Q, PACK, P], F32)
         nc.vector.tensor_tensor(ratio[:], papb[:], inv_den[:], ALU.mult)
         db = tile("db", [Q, PACK, P], F32)
         nc.vector.scalar_tensor_tensor(db[:], dealt(c0_ps), -1.0, ratio[:], ALU.mult, ALU.mult)
-
         dbt_ps = ps.tile([P, PACK, Q], F32, name="dbt_ps")
         for r in range(PACK):
             nc.tensor.transpose(dbt_ps[:, r, :], db[:, r, :], ident[:])
+
+        turn_keyrows(1, kr_pools[1], kt01_bf[:, P:, :], tag="ratio")
+
         gt_bf = tile("gt_bf", [P, Q, PACK], BF16)
         nc.vector.tensor_tensor(gt_bf[:], dbt_ps[:].rearrange("p r q -> p q r"),
                                 slot_w[:].unsqueeze(1).to_broadcast([P, Q, PACK]), ALU.mult)
+        kt2_bf = tile("kt2_bf", [P, P, PACK], BF16)
+        turn_keyrows(2, kr_pools[2], kt2_bf[:], at=AT_VS_POOL)
         gt_mx = quantise("gt", gt_bf)
+        kt3_bf = tile("kt3_bf", [P, P, PACK], BF16)
+        turn_keyrows(3, kr_pools[3], kt3_bf[:], tag="gt_bf")
+        kt01_mx = quantise("kt01", kt01_bf, at=AT_KR[3])
+        kt2_mx = quantise("kt2", kt2_bf, at=AT_KR[3] + 4 * I)
+        kt3_mx = quantise("kt3", kt3_bf)
 
-        for c in range(CHUNKS):
-            cols = slice(c * P, (c + 1) * P)
-            pairs = gather(f"kr{c}", kr_pools[c], BF16)[:].bitcast(F32)
-            kt_ps = ps.tile([P, 2, P], F32, name="kt_ps", bufs=2)
-            for u in range(2):
-                nc.tensor.transpose(kt_ps[:, u, :], pairs[:, u:I // 2:2], ident[:])
-            kt_bf = tile(f"kt_bf{c}", [P, P, PACK], BF16)
-            nc.scalar.copy(kt_bf[:].bitcast(F32), kt_ps[:].rearrange("p u d -> p d u"))
-            kt_mx = quantise(f"kt{c}", kt_bf)
-            gq_ps = ps.tile([Q, P], F32, name="gq_ps", bufs=2)
-            nc.tensor.matmul_mx(out=gq_ps[:], lhsT=gt_mx[0][:].bitcast(FP8X4), lhsT_scale=gt_mx[1][:],
-                                rhs=kt_mx[0][:].bitcast(FP8X4), rhs_scale=kt_mx[1][:], start=True, stop=True)
-            y = tile(f"y{c}", [Q, P], F32)
-            nc.vector.tensor_tensor(y[:], gq_ps[:], res_sb[:, cols], ALU.add)
-            nc.sync.dma_start(out[:, cols], y[:])
+        for name, first, parts in (("early", 0, (kt01_mx, kt2_mx)), ("last", D - P, (kt3_mx,))):
+            width = sum(codes.shape[1] for codes, scales in parts)
+            gq_ps = ps.tile([Q, width], F32, name="gq_" + name)
+            done = 0
+            for codes, scales in parts:
+                nc.tensor.matmul_mx(out=gq_ps[:, done:done + codes.shape[1]], lhsT=gt_mx[0][:].bitcast(FP8X4),
+                                    lhsT_scale=gt_mx[1][:], rhs=codes[:].bitcast(FP8X4), rhs_scale=scales[:],
+                                    start=True, stop=True)
+                done += codes.shape[1]
+            y = tile("y_" + name, [Q, width], F32)
+            nc.vector.tensor_tensor(y[:], gq_ps[:], res_sb[:, first:first + width], ALU.add)
+            nc.sync.dma_start(out[:, first:first + width], y[:])

@@ -23,7 +23,8 @@ CHUNKS = D // P
 POOL_BYTES = 4 * T
 ROWS_BYTES = 4 * I
 AT_KR0 = 0
-AT_KR1 = AT_KR0 + POOL_BYTES
+AT_VS_POOL = AT_KR0 + POOL_BYTES
+AT_KR1 = AT_VS_POOL + T
 AT_KR2 = AT_KR1 + POOL_BYTES
 AT_PB = AT_KR2 + POOL_BYTES
 AT_KR3 = AT_PB + ROWS_BYTES
@@ -33,8 +34,7 @@ AT_GO = AT_PB - ROWS_BYTES // 2
 AT_GO_BF = AT_KR3 + POOL_BYTES - I
 AT_VW_POOL = AT_GO_BF + 2 * I
 AT_VS = AT_VW_POOL - I // 2
-AT_VS_POOL = AT_VW_POOL + 2 * T
-AT_SIZE = AT_VS_POOL + T
+AT_SIZE = AT_VW_POOL + 2 * T
 AT_FS = AT_SIZE + 64
 AT_L2 = AT_FS + 64
 AT_L1 = AT_L2 + 64
@@ -145,8 +145,8 @@ def tile_attend_bclippedratio_b_q_kernel(tc, query, query2, keys_words, keys_sca
         nc.gpsimd.tensor_tensor(neg_l12[:], neg_l2[:], l1_col[:], ALU.subtract)
 
         kw = gather("kw", kw_pool, U16)
-        ks = gather("ks", ks_pool, U8)
         q2_mx = quantise("q2", interleave("q2_bf", q2_raw))
+        ks = gather("ks", ks_pool, U8, tag="q2_bf")
         q1_mx = quantise("q1", interleave("q1_bf", q1_raw))
         kr_pools.append(load_keyrows(1, at=AT_KR[1]))
 
@@ -161,8 +161,8 @@ def tile_attend_bclippedratio_b_q_kernel(tc, query, query2, keys_words, keys_sca
         kr_pools.append(load_keyrows(3, at=AT_KR[3]))
         vw = gather("vw", vw_pool, U16, tag="q1_bf")
         vs = gather("vs", vs_pool, U8, at=AT_VS)
-        slot_w = tile("slot_w", [P, PACK], F32, at=AT_VS_POOL)
-        nc.vector.tensor_tensor(slot_w[:], size_col[:], fs_col[:], ALU.mult)
+        slot_w = tile("slot_w", [P, PACK], F32)
+        nc.gpsimd.tensor_tensor(slot_w[:], size_col[:], fs_col[:], ALU.mult)
         c0_ps = ps.tile([Q, I], F32, name="c0_ps")
         score(c0_ps, go_mx, vw, vs, True, True)
 
@@ -182,26 +182,26 @@ def tile_attend_bclippedratio_b_q_kernel(tc, query, query2, keys_words, keys_sca
 
         kt01_bf = tile("kt01_bf", [P, 2 * P, PACK], BF16, at=AT_INV_ABS)
         turn_keyrows(0, kr_pools[0], kt01_bf[:, :P, :])
+        turn_keyrows(1, kr_pools[1], kt01_bf[:, P:, :], at=AT_KR[0])
 
-        ratio = tile("ratio", [Q, PACK, P], F32)
-        nc.vector.tensor_tensor(ratio[:], papb[:], inv_den[:], ALU.mult)
+        numer = tile("numer", [Q, PACK, P], F32, at=AT_KR[1])
+        nc.vector.scalar_tensor_tensor(numer[:], dealt(c0_ps), -1.0, papb[:], ALU.mult, ALU.mult)
         db = tile("db", [Q, PACK, P], F32)
-        nc.vector.scalar_tensor_tensor(db[:], dealt(c0_ps), -1.0, ratio[:], ALU.mult, ALU.mult)
+        nc.vector.tensor_tensor(db[:], numer[:], inv_den[:], ALU.mult)
         dbt_ps = ps.tile([P, PACK, Q], F32, name="dbt_ps")
         for r in range(PACK):
             nc.tensor.transpose(dbt_ps[:, r, :], db[:, r, :], ident[:])
 
-        turn_keyrows(1, kr_pools[1], kt01_bf[:, P:, :], tag="ratio")
+        kt2_bf = tile("kt2_bf", [P, P, PACK], BF16)
+        turn_keyrows(2, kr_pools[2], kt2_bf[:])
 
-        gt_bf = tile("gt_bf", [P, Q, PACK], BF16)
+        gt_bf = tile("gt_bf", [P, Q, PACK], BF16, at=AT_KR[2])
         nc.vector.tensor_tensor(gt_bf[:], dbt_ps[:].rearrange("p r q -> p q r"),
                                 slot_w[:].unsqueeze(1).to_broadcast([P, Q, PACK]), ALU.mult)
-        kt2_bf = tile("kt2_bf", [P, P, PACK], BF16)
-        turn_keyrows(2, kr_pools[2], kt2_bf[:], at=AT_VS_POOL)
-        gt_mx = quantise("gt", gt_bf)
         kt3_bf = tile("kt3_bf", [P, P, PACK], BF16)
-        turn_keyrows(3, kr_pools[3], kt3_bf[:], tag="gt_bf")
-        kt01_mx = quantise("kt01", kt01_bf, at=AT_KR[3])
+        turn_keyrows(3, kr_pools[3], kt3_bf[:])
+        gt_mx = quantise("gt", gt_bf, at=AT_KR[3])
+        kt01_mx = quantise("kt01", kt01_bf, at=AT_KR[3] + 2 * I)
         kt2_mx = quantise("kt2", kt2_bf, at=AT_KR[3] + 4 * I)
         kt3_mx = quantise("kt3", kt3_bf)
 

@@ -192,17 +192,19 @@ def tile_attend_bclippedratio_b_q_kernel(tc, query, query2, keys_words, keys_sca
         for r in range(PACK):
             nc.tensor.transpose(dbt_ps[:, r, :], db[:, r, :], ident[:])
 
+        gt_rows = tile("gt_rows", [P, PACK, Q], BF16)
+        for r in range(PACK):
+            nc.scalar.activation(gt_rows[:, r, :], dbt_ps[:, r, :], ACT.Copy, scale=slot_w[:, r:r + 1])
+        gt_bf = tile("gt_bf", [P, Q, PACK], BF16)
+        nc.scalar.copy(gt_bf[:], gt_rows[:].rearrange("p r q -> p q r"))
+
         kt2_bf = tile("kt2_bf", [P, P, PACK], BF16)
         turn_keyrows(2, kr_pools[2], kt2_bf[:])
-
-        gt_bf = tile("gt_bf", [P, Q, PACK], BF16, at=AT_KR[2])
-        nc.vector.tensor_tensor(gt_bf[:], dbt_ps[:].rearrange("p r q -> p q r"),
-                                slot_w[:].unsqueeze(1).to_broadcast([P, Q, PACK]), ALU.mult)
         kt3_bf = tile("kt3_bf", [P, P, PACK], BF16)
         turn_keyrows(3, kr_pools[3], kt3_bf[:])
-        gt_mx = quantise("gt", gt_bf, at=AT_KR[3])
-        kt01_mx = quantise("kt01", kt01_bf, at=AT_KR[3] + 2 * I)
-        kt2_mx = quantise("kt2", kt2_bf, at=AT_KR[3] + 4 * I)
+        kt01_mx = quantise("kt01", kt01_bf, at=AT_KR[3])
+        kt2_mx = quantise("kt2", kt2_bf, at=AT_KR[3] + 2 * I)
+        gt_mx = quantise("gt", gt_bf, at=AT_KR[3] + 4 * I)
         kt3_mx = quantise("kt3", kt3_bf)
 
         for name, first, parts in (("early", 0, (kt01_mx, kt2_mx)), ("last", D - P, (kt3_mx,))):

from contextlib import ExitStack

import concourse.mybir as mybir

D, E, T, I, Q = 512, 512, 2048, 512, 128
FLOPS = 2 * Q * I * (D + D + E + D)

F32 = mybir.dt.float32
BF16 = mybir.dt.bfloat16
I32 = mybir.dt.int32
U32 = mybir.dt.uint32
U16 = mybir.dt.uint16
U8 = mybir.dt.uint8
FP8X4 = mybir.dt.float8_e4m3fn_x4
FP4X4 = mybir.dt.float4_e2m1fn_x4
ACT = mybir.ActivationFunctionType
ALU = mybir.AluOpType

P = 128
PACK = 4
CHUNKS = D // P

POOL_BYTES = 4 * T
ROWS_BYTES = 4 * I
AT_KR0 = 0
AT_VS_POOL = AT_KR0 + POOL_BYTES
AT_KR1 = AT_VS_POOL + T
AT_KR2 = AT_KR1 + POOL_BYTES
AT_PB = AT_KR2 + POOL_BYTES
AT_KR3 = AT_PB + ROWS_BYTES
AT_KR = [AT_KR0, AT_KR1, AT_KR2, AT_KR3]
AT_Q1 = AT_KR1
AT_GO = AT_PB - ROWS_BYTES // 2
AT_GO_BF = AT_KR3 + POOL_BYTES - I
AT_VW_POOL = AT_GO_BF + 2 * I
AT_VS = AT_VW_POOL - I // 2
AT_SIZE = AT_VW_POOL + 2 * T
AT_FS = AT_SIZE + 64
AT_L2 = AT_FS + 64
AT_L1 = AT_L2 + 64
AT_FLOOR = AT_L1 + 64
STAGED_BYTES = AT_FLOOR + 64
AT_INV_ABS = STAGED_BYTES


def tile_attend_bclippedratio_b_q_kernel(tc, query, query2, keys_words, keys_scales, l1, l2, floor, gout,
                                          vals_words, vals_scales, size, fs, keyrows, res, offs, out):
    nc = tc.nc
    with ExitStack() as ctx:
        sb = ctx.enter_context(tc.tile_pool(name="sb", bufs=1))
        staged = ctx.enter_context(tc.tile_pool(name="staged", bufs=1))
        ps = ctx.enter_context(tc.psum_pool(name="ps", bufs=1))

        def tile(name, shape, dtype, tag=None, at=None):
            if at is None:
                return sb.tile(shape, dtype, name=name, tag=tag or name, align_bytes=64)
            return staged.tile(shape, dtype, name=name, align_bytes=64, offset=at)

        offsets = sb.tile([P, I // 16], U16, name="offsets")
        nc.sync.dma_start(offsets[:], offs)

        def load_scales(name, scales, zeroing, **place):
            plane = tile(name, [P, T], U8, **place)
            zeroing.memset(plane[:].bitcast(I32), 0)
            for r in range(4):
                nc.sync.dma_start(plane[r:P:32, :].bitcast(I32), scales[0, r:16:4, :].bitcast(I32))
            return plane

        def load_words(name, words, **place):
            pool = tile(name, [P, T], U16, **place)
            nc.sync.dma_start(pool[:].bitcast(I32), words[0].bitcast(I32))
            return pool

        def load_columns(name, src, **place):
            raw = tile(name, [P, PACK, Q], F32, **place)
            nc.sync.dma_start(raw[:], src.rearrange("(p j) q -> p j q", j=PACK))
            return raw

        def load_small(name, src, queue, **place):
            small = tile(name, list(src.shape), F32, **place)
            queue.dma_start(small[:], src)
            return small

        def load_keyrows(c, **place):
            pool = tile(f"kr_pool{c}", [P, T], F32, **place)
            nc.sync.dma_start(pool[:], keyrows[c * P:(c + 1) * P, :])
            return pool

        def gather(name, pool, dtype, **place):
            picked = tile(name, [P, I], dtype, **place)
            nc.vector.tensor_copy(picked[:], pool[:].indirect(offsets[:]))
            return picked

        def interleave(name, raw, **place):
            grouped = tile(name, [P, Q, PACK], BF16, **place)
            nc.scalar.activation(grouped[:], raw[:].rearrange("p j q -> p q j"), ACT.Copy)
            return grouped

        def quantise(name, grouped, at=None):
            width = grouped.shape[1]
            codes = tile(name + "_codes", [P, width], U32, at=at)
            scales = tile(name + "_scales", [P, width], U8)
            nc.vector.quantize_mx(out=codes[:].bitcast(FP8X4), scales=scales[:],
                                  in_=grouped[:].rearrange("p c j -> p (c j)"))
            return codes, scales

        def score(bank, rows, words, scales, start, stop):
            nc.tensor.matmul_mx(out=bank[:], lhsT=rows[0][:].bitcast(FP8X4), lhsT_scale=rows[1][:],
                                rhs=words[:].bitcast(FP4X4), rhs_scale=scales[:], start=start, stop=stop)

        def dealt(bank):
            return bank[:].rearrange("q (s r) -> q r s", r=PACK)

        def turn_keyrows(c, pool, grouped, **place):
            pairs = gather(f"kr{c}", pool, BF16, **place)[:].bitcast(F32)
            kt_ps = ps.tile([P, 2, P], F32, name="kt_ps", bufs=2)
            for u in range(2):
                nc.tensor.transpose(kt_ps[:, u, :], pairs[:, u:I // 2:2], ident[:])
            nc.scalar.copy(grouped.bitcast(F32), kt_ps[:].rearrange("p u d -> p d u"))

        kw_pool = load_words("kw_pool", keys_words)
        q2_raw = load_columns("q2_raw", query2)
        zeros = tile("zeros", [P, STAGED_BYTES // 4], F32, at=0)
        nc.vector.memset(zeros[:, :P], 0.0)
        ident = tile("ident", [P, P], F32)
        nc.gpsimd.affine_select(out=ident[:], in_=zeros[:, :P], compare_op=ALU.not_equal, fill=1.0, base=0,
                                pattern=[[-1, P]], channel_multiplier=1)

        ks_pool = load_scales("ks_pool", keys_scales, nc.vector)

        q1_raw = load_columns("q1_raw", query, at=AT_Q1)
        go_raw = load_columns("go_raw", gout, at=AT_GO)
        vw_pool = load_words("vw_pool", vals_words, at=AT_VW_POOL)
        l2_col = load_small("l2_col", l2, nc.sync, at=AT_L2)
        l1_col = load_small("l1_col", l1, nc.sync, at=AT_L1)
        floor_col = load_small("floor_col", floor, nc.sync, at=AT_FLOOR)
        kr_pools = [load_keyrows(0, at=AT_KR[0])]
        vs_pool = load_scales("vs_pool", vals_scales, nc.gpsimd, at=AT_VS_POOL)
        size_col = load_small("size_col", size.rearrange("o (p r) -> (o p) r", r=PACK), nc.sync, at=AT_SIZE)
        fs_col = load_small("fs_col", fs.rearrange("o (p r) -> (o p) r", r=PACK), nc.sync, at=AT_FS)

        neg_l2 = tile("neg_l2", [Q, 1], F32)
        nc.gpsimd.tensor_scalar(neg_l2[:], l2_col[:], -1.0, 0.0, ALU.mult, ALU.add)
        neg_l12 = tile("neg_l12", [Q, 1], F32, at=AT_INV_ABS)
        nc.gpsimd.tensor_tensor(neg_l12[:], neg_l2[:], l1_col[:], ALU.subtract)

        kw = gather("kw", kw_pool, U16)
        q2_mx = quantise("q2", interleave("q2_bf", q2_raw))
        ks = gather("ks", ks_pool, U8, tag="q2_bf")
        q1_mx = quantise("q1", interleave("q1_bf", q1_raw))
        kr_pools.append(load_keyrows(1, at=AT_KR[1]))

        b_ps = ps.tile([Q, I], F32, name="b_ps")
        ab_ps = ps.tile([Q, I], F32, name="ab_ps")
        score(b_ps, q2_mx, kw, ks, True, True)
        score(ab_ps, q2_mx, kw, ks, True, False)
        score(ab_ps, q1_mx, kw, ks, False, True)

        go_mx = quantise("go", interleave("go_bf", go_raw, at=AT_GO_BF))
        kr_pools.append(load_keyrows(2, at=AT_KR[2]))
        kr_pools.append(load_keyrows(3, at=AT_KR[3]))
        vw = gather("vw", vw_pool, U16, tag="q1_bf")
        vs = gather("vs", vs_pool, U8, at=AT_VS)
        slot_w = tile("slot_w", [P, PACK], F32)
        nc.gpsimd.tensor_tensor(slot_w[:], size_col[:], fs_col[:], ALU.mult)
        c0_ps = ps.tile([Q, I], F32, name="c0_ps")
        score(c0_ps, go_mx, vw, vs, True, True)

        res_sb = tile("res_sb", [Q, D], F32, tag="go_codes")
        nc.sync.dma_start(res_sb[:], res)

        pb = tile("pb", [Q, PACK, P], F32, at=AT_PB)
        nc.scalar.activation(pb[:], dealt(b_ps), ACT.Exp, bias=neg_l2[:])
        papb = tile("papb", [Q, PACK, P], F32)
        nc.scalar.activation(papb[:], dealt(ab_ps), ACT.Exp, bias=neg_l12[:])
        den = tile("den", [Q, PACK, P], F32)
        nc.scalar.activation(den[:], pb[:], ACT.Square, bias=floor_col[:])
        inv_abs = tile("inv_abs", [Q, PACK, P], F32, at=AT_INV_ABS)
        nc.scalar.activation(inv_abs[:], den[:], ACT.Abs_reciprocal_sqrt)
        inv_den = tile("inv_den", [Q, PACK, P], F32)
        nc.scalar.activation(inv_den[:], inv_abs[:], ACT.Square)

        kt01_bf = tile("kt01_bf", [P, 2 * P, PACK], BF16, at=AT_INV_ABS)
        turn_keyrows(0, kr_pools[0], kt01_bf[:, :P, :])
        turn_keyrows(1, kr_pools[1], kt01_bf[:, P:, :], at=AT_KR[0])

        numer = tile("numer", [Q, PACK, P], F32, at=AT_KR[1])
        nc.vector.scalar_tensor_tensor(numer[:], dealt(c0_ps), -1.0, papb[:], ALU.mult, ALU.mult)
        db = tile("db", [Q, PACK, P], F32)
        nc.vector.tensor_tensor(db[:], numer[:], inv_den[:], ALU.mult)
        dbt_ps = ps.tile([P, PACK, Q], F32, name="dbt_ps")
        for r in range(PACK):
            nc.tensor.transpose(dbt_ps[:, r, :], db[:, r, :], ident[:])

        gt_rows = tile("gt_rows", [P, PACK, Q], BF16)
        for r in range(PACK):
            nc.scalar.activation(gt_rows[:, r, :], dbt_ps[:, r, :], ACT.Copy, scale=slot_w[:, r:r + 1])
        gt_bf = tile("gt_bf", [P, Q, PACK], BF16)
        nc.scalar.copy(gt_bf[:], gt_rows[:].rearrange("p r q -> p q r"))

        kt2_bf = tile("kt2_bf", [P, P, PACK], BF16)
        turn_keyrows(2, kr_pools[2], kt2_bf[:])
        kt3_bf = tile("kt3_bf", [P, P, PACK], BF16)
        turn_keyrows(3, kr_pools[3], kt3_bf[:])
        kt01_mx = quantise("kt01", kt01_bf, at=AT_KR[3])
        kt2_mx = quantise("kt2", kt2_bf, at=AT_KR[3] + 2 * I)
        gt_mx = quantise("gt", gt_bf, at=AT_KR[3] + 4 * I)
        kt3_mx = quantise("kt3", kt3_bf)

        for name, first, parts in (("early", 0, (kt01_mx, kt2_mx)), ("last", D - P, (kt3_mx,))):
            width = sum(codes.shape[1] for codes, scales in parts)
            gq_ps = ps.tile([Q, width], F32, name="gq_" + name)
            done = 0
            for codes, scales in parts:
                nc.tensor.matmul_mx(out=gq_ps[:, done:done + codes.shape[1]], lhsT=gt_mx[0][:].bitcast(FP8X4),
                                    lhsT_scale=gt_mx[1][:], rhs=codes[:].bitcast(FP8X4), rhs_scale=scales[:],
                                    start=True, stop=True)
                done += codes.shape[1]
            y = tile("y_" + name, [Q, width], F32)
            nc.vector.tensor_tensor(y[:], gq_ps[:], res_sb[:, first:first + width], ALU.add)
            nc.sync.dma_start(out[:, first:first + width], y[:])
